import numpy as np
import ml_dtypes


def mxq(x, axis, fmt="e4m3"):
    dtype, down = {"e4m3": (ml_dtypes.float8_e4m3fn, 7), "e5m2": (ml_dtypes.float8_e5m2, 14)}[fmt]
    v = np.moveaxis(np.asarray(x, np.float32).astype(ml_dtypes.bfloat16).astype(np.float64), axis, -1)
    blocks = v.reshape(v.shape[:-1] + (-1, 32))
    amax = np.abs(blocks).max(-1, keepdims=True)
    byte = np.maximum(np.where(amax > 0, np.frexp(amax)[1] - 1 + 127, 0) - down, 1)
    scale = np.exp2(byte - 127.0)
    codes = (blocks / scale).astype(np.float32).astype(dtype).astype(np.float64)
    return np.moveaxis((codes * scale).reshape(v.shape), -1, axis)


WIDE = False


def mx_kscale(k):
    if not WIDE:
        return np.ones(k)
    levels = np.array([10, -10, 5, -5, 0])
    if k % 512:
        return np.exp2(np.random.permutation(np.resize(levels, k // 32))).repeat(32)
    a = np.empty((k // 512, 16))
    for p in range(k // 512):
        a[p, :8] = np.random.permutation(np.resize(levels, 8))
        for g in range(8):
            far = levels[np.abs(levels - a[p, g]) >= 10]
            a[p, g + 8] = far[np.random.randint(len(far))]
    return np.exp2(a.ravel()).repeat(32)


def f64(x):
    return np.asarray(x).astype(np.float64)


def striped(idx):
    return np.tile(np.asarray(idx).reshape(-1, 16).T, (8, 1)).astype(np.uint16)


def unstriped(offs):
    return offs[:16].T.reshape(-1).astype(np.int64)


E2M1 = np.array([0.0, 0.5, 1.0, 1.5, 2.0, 3.0, 4.0, 6.0, -0.0, -0.5, -1.0, -1.5, -2.0, -3.0, -4.0, -6.0])


def pack_weight(w, fmt):
    k, n = w.shape
    w = f64(np.asarray(w, np.float32).astype(ml_dtypes.bfloat16)).reshape(k // 32, 32, n)
    amax = np.abs(w).max(1)
    if fmt == "e4m3":
        byte = np.frexp(amax)[1] - 1 + 127 - 7
    else:
        mant, ex = np.frexp(amax / 6.0)
        byte = np.where(mant > 0.5, ex, ex - 1) + 127
    byte = np.clip(np.where(amax > 0, byte, 1), 1, 254)
    scaled = (w * np.exp2(127.0 - byte)[:, None, :]).reshape(k, n).astype(np.float32)
    by_word = np.ascontiguousarray(scaled.reshape(k // 512, 128, 4, n).transpose(0, 1, 3, 2))
    if fmt == "e4m3":
        words = by_word.astype(ml_dtypes.float8_e4m3fn).view(np.uint8)
    else:
        c = by_word.astype(ml_dtypes.float4_e2m1fn).view(np.uint8) & 0xF
        words = (c[..., 0::2] | (c[..., 1::2] << 4)).reshape(k // 512, 128, 2 * n)
    return np.ascontiguousarray(words), np.ascontiguousarray(byte.astype(np.uint8).reshape(k // 512, 16, n))


def unpack_weight(words, scales, fmt):
    g, _, n = scales.shape
    words = np.ascontiguousarray(words).reshape(g, 128, n, -1)
    if fmt == "e4m3":
        vals = words.view(ml_dtypes.float8_e4m3fn).astype(np.float64)
    else:
        nib = np.empty((g, 128, n, 4), np.uint8)
        nib[..., 0::2] = words & 0xF
        nib[..., 1::2] = words >> 4
        vals = E2M1[nib]
    vals = vals * np.repeat(np.exp2(scales.astype(np.float64) - 127.0), 8, axis=1)[..., None]
    return vals.transpose(0, 1, 3, 2).reshape(g * 512, n)


def e4m3fn_bytes(y):
    return np.clip(np.asarray(y, np.float64), -448.0, 448.0).astype(np.float32).astype(ml_dtypes.float8_e4m3fn).view(np.uint8)


def e4m3fn_values(b):
    return np.asarray(b, np.uint8).view(ml_dtypes.float8_e4m3fn).astype(np.float64)


K, T, J, R, D, U, O = 512, 1024, 256, 512, 2048, 512, 256


def setup_inputs():
    n = np.random.standard_normal
    idx = np.random.permutation(T)[:J]
    idx2 = np.random.permutation(D)[:U]
    idx3 = np.random.permutation(U)[:O]
    fk = mx_kscale(K)
    fr = mx_kscale(R)
    xtp = pack_weight(n((K, T)) / fk[:, None], "e4m3")
    wp = pack_weight(n((K, R)) * 1 / np.sqrt(K) * fk[:, None] * fr, "e2m1")
    return {
        "xt_words": xtp[0],
        "xt_scales": xtp[1],
        "w_words": wp[0],
        "w_scales": wp[1],
        "ca": e4m3fn_bytes(60.0 * n((R, D))),
        "st": (np.random.uniform(0.0002, 0.0006, (R, 1)) / fr[:, None]).astype(np.float32),
        "offs": striped(idx),
        "offs2": striped(idx2),
        "offs3": striped(idx3),
    }


def reference(xt_words, xt_scales, w_words, w_scales, ca, st, offs, offs2, offs3):
    idx = unstriped(offs)
    idx2 = unstriped(offs2)
    idx3 = unstriped(offs3)
    xtu = unpack_weight(xt_words, xt_scales, "e4m3")
    wu = unpack_weight(w_words, w_scales, "e2m1")
    xtidxg = xtu[:, idx]
    a = wu.T @ xtidxg
    k1 = e4m3fn_values(ca)[:, idx2] * f64(st)
    kp = k1[:, idx3]
    aq = mxq(a, 0, "e4m3")
    kpq = mxq(kp, 0, "e4m3")
    p = aq.T @ kpq
    return p

@@ -1,0 +1,163 @@
+from contextlib import ExitStack
+
+import concourse.mybir as mybir
+
+K, T, J, R, D, U, O = 512, 1024, 256, 512, 2048, 512, 256
+FLOPS = 2 * K * R * J + 2 * R * J * O
+
+F32 = mybir.dt.float32
+BF16 = mybir.dt.bfloat16
+I32 = mybir.dt.int32
+U32 = mybir.dt.uint32
+U16 = mybir.dt.uint16
+U8 = mybir.dt.uint8
+FP8 = mybir.dt.float8_e4m3fn
+FP8X4 = mybir.dt.float8_e4m3fn_x4
+FP4X4 = mybir.dt.float4_e2m1fn_x4
+COPY = mybir.ActivationFunctionType.Copy
+
+P = 128
+PACK = 4
+HALF = 128
+
+
+def tile_list_twolevels_kernel(tc, xt_words, xt_scales, w_words, w_scales, ca, st, offs, offs2, offs3, out):
+    nc = tc.nc
+    with ExitStack() as ctx:
+        lists = ctx.enter_context(tc.tile_pool(name="lists", bufs=1))
+        keep = ctx.enter_context(tc.tile_pool(name="keep", bufs=1))
+        psum = ctx.enter_context(tc.psum_pool(name="psum", bufs=1))
+
+        offs_sb = lists.tile([P, J // 16], U16, name="offs_sb")
+        offs2_sb = lists.tile([P, U // 16], U16, name="offs2_sb")
+        offs3_sb = lists.tile([P, O // 16], U16, name="offs3_sb")
+
+        ca_sb = [keep.tile([P, D], U8, name=f"ca_sb{t}") for t in range(PACK)]
+        ca_picked = [keep.tile([P, U], U8, name=f"ca_picked{t}") for t in range(PACK)]
+        k1 = [keep.tile([P, U], F32, name=f"k1_{t}") for t in range(PACK)]
+        st_sb = keep.tile([P, PACK], F32, name="st_sb")
+        xw_sb = keep.tile([P, T], I32, name="xw_sb")
+        xs_sb = keep.tile([P, T], U8, name="xs_sb")
+        xw_picked = keep.tile([P, J], U32, name="xw_picked", align_bytes=64)
+        xs_picked = keep.tile([P, J], U8, name="xs_picked", align_bytes=64)
+        ww_sb = keep.tile([P, 2 * R], U8, name="ww_sb")
+        ws_sb = keep.tile([P, R], U8, name="ws_sb")
+        ww_dealt = keep.tile([P, 2 * R], U8, name="ww_dealt", align_bytes=64)
+        ws_dealt = keep.tile([P, R], U8, name="ws_dealt", align_bytes=64)
+        a_bf = [keep.tile([P, HALF, PACK], BF16, name=f"a_bf{h}", align_bytes=64) for h in range(2)]
+        a_codes = [keep.tile([P, HALF], U32, name=f"a_codes{h}", align_bytes=64) for h in range(2)]
+        a_scales = [keep.tile([P, HALF], U8, name=f"a_scales{h}", align_bytes=64) for h in range(2)]
+        kp_bf = keep.tile([P, O * PACK], BF16, name="kp_bf", align_bytes=64)
+        kp_codes = [keep.tile([P, HALF], U32, name=f"kp_codes{h}", align_bytes=64) for h in range(2)]
+        kp_scales = [keep.tile([P, HALF], U8, name=f"kp_scales{h}", align_bytes=64) for h in range(2)]
+        out_sb = [keep.tile([P, O], F32, name=f"out_sb{h}") for h in range(2)]
+        a_ps = [psum.tile([P, PACK, HALF], F32, name=f"a_ps{h}") for h in range(2)]
+        out_ps = [psum.tile([P, O], F32, name=f"out_ps{h}") for h in range(2)]
+
+        ca_rows = ca.rearrange("(p t) d -> t p d", t=PACK)
+
+        def load_scale_rows(queue, plane, rows):
+            for r in range(4):
+                queue.dma_start(out=plane[r:P:32, :].bitcast(I32), in_=rows[0, r:16:4, :].bitcast(I32))
+
+        nc.vector.memset(ws_sb[:].bitcast(I32), 0)
+        nc.vector.memset(xs_sb[:].bitcast(I32), 0)
+
+        nc.sync.dma_start(offs2_sb[:], offs2)
+        nc.sync.dma_start(out=ca_sb[0][:], in_=ca_rows[0])
+        load_scale_rows(nc.scalar, ws_sb, w_scales)
+        nc.sync.dma_start(out=ca_sb[1][:], in_=ca_rows[1])
+        nc.sync.dma_start(out=ww_sb[:].bitcast(I32), in_=w_words[0].bitcast(I32))
+        nc.sync.dma_start(out=st_sb[:], in_=st.rearrange("(p t) o -> p (t o)", t=PACK))
+        nc.sync.dma_start(offs3_sb[:], offs3)
+        nc.sync.dma_start(offs_sb[:], offs)
+        nc.sync.dma_start(out=xw_sb[:], in_=xt_words[0].rearrange("p n t -> p (n t)").bitcast(I32))
+        load_scale_rows(nc.sync, xs_sb, xt_scales)
+        nc.sync.dma_start(out=ca_sb[2][:], in_=ca_rows[2])
+        nc.sync.dma_start(out=ca_sb[3][:], in_=ca_rows[3])
+
+        nc.vector.tensor_copy(
+            out=ws_dealt[:].rearrange("p (t m) -> p t m", t=PACK),
+            in_=ws_sb[:].rearrange("p (m t) -> p t m", t=PACK),
+        )
+        nc.scalar.copy(
+            out=ww_dealt[:].bitcast(U16).rearrange("p (t m) -> p t m", t=PACK),
+            in_=ww_sb[:].bitcast(U16).rearrange("p (m t) -> p t m", t=PACK),
+        )
+
+        def pick_codes(t, lo, hi):
+            nc.vector.tensor_copy(out=ca_picked[t][:, lo:hi], in_=ca_sb[t][:].indirect(offs2_sb[:, lo // 16 : hi // 16]))
+
+        def make_k1(t, lo, hi):
+            nc.scalar.activation(out=k1[t][:, lo:hi], in_=ca_picked[t][:, lo:hi].bitcast(FP8), func=COPY, scale=st_sb[:, t : t + 1])
+
+        def kp_slot(t, lo, hi):
+            return kp_bf[:, PACK * lo + t : PACK * hi : PACK], k1[t][:].indirect(offs3_sb[:, lo // 16 : hi // 16])
+
+        def pick_kp_scalar(t, lo, hi):
+            slot, picked = kp_slot(t, lo, hi)
+            nc.scalar.activation(out=slot, in_=picked, func=COPY)
+
+        def pick_kp_vector(t, lo, hi):
+            slot, picked = kp_slot(t, lo, hi)
+            nc.vector.tensor_copy(out=slot, in_=picked)
+
+        for t in range(2):
+            pick_codes(t, 0, U)
+            make_k1(t, 0, U)
+            pick_kp_scalar(t, 0, O)
+
+        nc.vector.tensor_copy(out=xw_picked[:], in_=xw_sb[:].bitcast(U32).indirect(offs_sb[:]))
+        nc.vector.tensor_copy(out=xs_picked[:], in_=xs_sb[:].indirect(offs_sb[:]))
+        for h in range(2):
+            cols = slice(h * HALF, (h + 1) * HALF)
+            for t in range(PACK):
+                nc.tensor.matmul_mx(
+                    out=a_ps[h][:, t, :],
+                    lhsT=ww_dealt[:, 2 * P * t : 2 * P * (t + 1)].bitcast(FP4X4),
+                    lhsT_scale=ws_dealt[:, P * t : P * (t + 1)],
+                    rhs=xw_picked[:, cols].bitcast(FP8X4),
+                    rhs_scale=xs_picked[:, cols],
+                    start=True,
+                    stop=True,
+                )
+
+        pick_codes(2, 0, U)
+        pick_codes(3, 0, U // 2)
+        pick_codes(3, U // 2, U)
+
+        nc.scalar.copy(out=a_bf[0][:], in_=a_ps[0][:].rearrange("p t j -> p j t"))
+        make_k1(2, 0, U)
+        nc.scalar.copy(out=a_bf[1][:], in_=a_ps[1][:].rearrange("p t j -> p j t"))
+        make_k1(3, 0, U // 2)
+        make_k1(3, U // 2, U)
+        pick_kp_vector(2, HALF, O)
+        pick_kp_scalar(2, 0, HALF)
+        for h in range(2):
+            nc.vector.quantize_mx(
+                out=a_codes[h][:].bitcast(FP8X4), scales=a_scales[h][:], in_=a_bf[h][:].rearrange("p j t -> p (j t)")
+            )
+        pick_kp_vector(3, HALF, O)
+        pick_kp_scalar(3, 0, HALF)
+
+        for g in range(2):
+            nc.vector.quantize_mx(
+                out=kp_codes[g][:].bitcast(FP8X4),
+                scales=kp_scales[g][:],
+                in_=kp_bf[:, PACK * HALF * g : PACK * HALF * (g + 1)],
+            )
+            for h in range(2):
+                nc.tensor.matmul_mx(
+                    out=out_ps[h][:, g * HALF : (g + 1) * HALF],
+                    lhsT=a_codes[h][:].bitcast(FP8X4),
+                    lhsT_scale=a_scales[h][:],
+                    rhs=kp_codes[g][:].bitcast(FP8X4),
+                    rhs_scale=kp_scales[g][:],
+                    start=True,
+                    stop=True,
+                )
+
+        nc.scalar.copy(out=out_sb[0][:], in_=out_ps[0][:])
+        nc.scalar.dma_start(out=out[0:HALF, :], in_=out_sb[0][:])
+        nc.vector.tensor_copy(out=out_sb[1][:], in_=out_ps[1][:])
+        nc.sync.dma_start(out=out[HALF:J, :], in_=out_sb[1][:])

@@ -42,19 +42,22 @@ def tile_list_twolevels_kernel(tc, xt_words, xt_scales, w_words, w_scales, ca, s
         xs_picked = keep.tile([P, J], U8, name="xs_picked", align_bytes=64)
         ww_sb = keep.tile([P, 2 * R], U8, name="ww_sb")
         ws_sb = keep.tile([P, R], U8, name="ws_sb")
+        ws_rows = keep.tile([4, 4, R], U8, name="ws_rows")
         ww_dealt = keep.tile([P, 2 * R], U8, name="ww_dealt", align_bytes=64)
         ws_dealt = keep.tile([P, R], U8, name="ws_dealt", align_bytes=64)
         a_bf = [keep.tile([P, HALF, PACK], BF16, name=f"a_bf{h}", align_bytes=64) for h in range(2)]
         a_codes = [keep.tile([P, HALF], U32, name=f"a_codes{h}", align_bytes=64) for h in range(2)]
         a_scales = [keep.tile([P, HALF], U8, name=f"a_scales{h}", align_bytes=64) for h in range(2)]
-        kp_bf = keep.tile([P, O * PACK], BF16, name="kp_bf", align_bytes=64)
+        kp_planes = keep.tile([P, PACK, O], BF16, name="kp_planes")
+        kp_bf = [keep.tile([P, HALF, PACK], BF16, name=f"kp_bf{h}", align_bytes=64) for h in range(2)]
         kp_codes = [keep.tile([P, HALF], U32, name=f"kp_codes{h}", align_bytes=64) for h in range(2)]
         kp_scales = [keep.tile([P, HALF], U8, name=f"kp_scales{h}", align_bytes=64) for h in range(2)]
-        out_sb = [keep.tile([P, O], F32, name=f"out_sb{h}") for h in range(2)]
+        out_sb = [keep.tile([P, 2, HALF], F32, name=f"out_sb{g}") for g in range(2)]
         a_ps = [psum.tile([P, PACK, HALF], F32, name=f"a_ps{h}") for h in range(2)]
-        out_ps = [psum.tile([P, O], F32, name=f"out_ps{h}") for h in range(2)]
+        out_ps = [[psum.tile([P, HALF], F32, name=f"out_ps{g}{h}") for h in range(2)] for g in range(2)]
 
-        ca_rows = ca.rearrange("(p t) d -> t p d", t=PACK)
+        ca_rows = ca.rearrange("(c t e) d -> t c e d", t=PACK, e=2)
+        st_rows = st.rearrange("(c t e) o -> e c (t o)", t=PACK, e=2)
 
         def load_scale_rows(queue, plane, rows):
             for r in range(4):
@@ -64,25 +67,29 @@ def tile_list_twolevels_kernel(tc, xt_words, xt_scales, w_words, w_scales, ca, s
         nc.vector.memset(xs_sb[:].bitcast(I32), 0)
 
         nc.sync.dma_start(offs2_sb[:], offs2)
+        nc.scalar.dma_start(out=ws_rows[:].bitcast(I32), in_=w_scales[0].rearrange("(q r) c -> r q c", r=4).bitcast(I32))
         nc.sync.dma_start(out=ca_sb[0][:], in_=ca_rows[0])
-        load_scale_rows(nc.scalar, ws_sb, w_scales)
-        nc.sync.dma_start(out=ca_sb[1][:], in_=ca_rows[1])
         nc.sync.dma_start(out=ww_sb[:].bitcast(I32), in_=w_words[0].bitcast(I32))
-        nc.sync.dma_start(out=st_sb[:], in_=st.rearrange("(p t) o -> p (t o)", t=PACK))
+        nc.sync.dma_start(out=ca_sb[1][:], in_=ca_rows[1])
+        with nc.allow_non_contiguous_dma(reason="one step for each partition and plane"):
+            for e in range(2):
+                nc.sync.dma_start(out=st_sb[e:P:2, :], in_=st_rows[e])
         nc.sync.dma_start(offs3_sb[:], offs3)
-        nc.sync.dma_start(offs_sb[:], offs)
-        nc.sync.dma_start(out=xw_sb[:], in_=xt_words[0].rearrange("p n t -> p (n t)").bitcast(I32))
-        load_scale_rows(nc.sync, xs_sb, xt_scales)
         nc.sync.dma_start(out=ca_sb[2][:], in_=ca_rows[2])
+        nc.sync.dma_start(out=xw_sb[:], in_=xt_words[0].rearrange("p n t -> p (n t)").bitcast(I32))
+        nc.sync.dma_start(offs_sb[:], offs)
+        load_scale_rows(nc.sync, xs_sb, xt_scales)
         nc.sync.dma_start(out=ca_sb[3][:], in_=ca_rows[3])
 
-        nc.vector.tensor_copy(
-            out=ws_dealt[:].rearrange("p (t m) -> p t m", t=PACK),
-            in_=ws_sb[:].rearrange("p (m t) -> p t m", t=PACK),
+        for q in range(4):
+            nc.vector.tensor_copy(out=ws_sb[32 * q : 32 * q + 4, :].bitcast(I32), in_=ws_rows[:, q, :].bitcast(I32))
+        nc.scalar.copy(
+            out=ww_dealt[:].bitcast(U32).rearrange("p (t c) -> p t c", t=PACK),
+            in_=ww_sb[:].bitcast(U32).rearrange("p (c t) -> p t c", t=PACK),
         )
         nc.scalar.copy(
-            out=ww_dealt[:].bitcast(U16).rearrange("p (t m) -> p t m", t=PACK),
-            in_=ww_sb[:].bitcast(U16).rearrange("p (m t) -> p t m", t=PACK),
+            out=ws_dealt[:].bitcast(U16).rearrange("p (t c) -> p t c", t=PACK),
+            in_=ws_sb[:].bitcast(U16).rearrange("p (c t) -> p t c", t=PACK),
         )
 
         def pick_codes(t, lo, hi):
@@ -91,21 +98,13 @@ def tile_list_twolevels_kernel(tc, xt_words, xt_scales, w_words, w_scales, ca, s
         def make_k1(t, lo, hi):
             nc.scalar.activation(out=k1[t][:, lo:hi], in_=ca_picked[t][:, lo:hi].bitcast(FP8), func=COPY, scale=st_sb[:, t : t + 1])
 
-        def kp_slot(t, lo, hi):
-            return kp_bf[:, PACK * lo + t : PACK * hi : PACK], k1[t][:].indirect(offs3_sb[:, lo // 16 : hi // 16])
+        def pick_kp(t, lo, hi):
+            nc.scalar.activation(out=kp_planes[:, t, lo:hi], in_=k1[t][:].indirect(offs3_sb[:, lo // 16 : hi // 16]), func=COPY)
 
-        def pick_kp_scalar(t, lo, hi):
-            slot, picked = kp_slot(t, lo, hi)
-            nc.scalar.activation(out=slot, in_=picked, func=COPY)
-
-        def pick_kp_vector(t, lo, hi):
-            slot, picked = kp_slot(t, lo, hi)
-            nc.vector.tensor_copy(out=slot, in_=picked)
-
-        for t in range(2):
+        for t in range(3):
             pick_codes(t, 0, U)
             make_k1(t, 0, U)
-            pick_kp_scalar(t, 0, O)
+            pick_kp(t, 0, O)
 
         nc.vector.tensor_copy(out=xw_picked[:], in_=xw_sb[:].bitcast(U32).indirect(offs_sb[:]))
         nc.vector.tensor_copy(out=xs_picked[:], in_=xs_sb[:].indirect(offs_sb[:]))
@@ -122,33 +121,39 @@ def tile_list_twolevels_kernel(tc, xt_words, xt_scales, w_words, w_scales, ca, s
                     stop=True,
                 )
 
-        pick_codes(2, 0, U)
         pick_codes(3, 0, U // 2)
         pick_codes(3, U // 2, U)
 
-        nc.scalar.copy(out=a_bf[0][:], in_=a_ps[0][:].rearrange("p t j -> p j t"))
-        make_k1(2, 0, U)
-        nc.scalar.copy(out=a_bf[1][:], in_=a_ps[1][:].rearrange("p t j -> p j t"))
-        make_k1(3, 0, U // 2)
-        make_k1(3, U // 2, U)
-        pick_kp_vector(2, HALF, O)
-        pick_kp_scalar(2, 0, HALF)
+        for h in range(2):
+            nc.scalar.copy(out=a_bf[h][:], in_=a_ps[h][:].rearrange("p t j -> p j t"))
+        for lo in (0, U // 2):
+            nc.vector.tensor_scalar(
+                out=k1[3][:, lo : lo + U // 2],
+                in0=ca_picked[3][:, lo : lo + U // 2].bitcast(FP8),
+                scalar1=st_sb[:, 3:4],
+                scalar2=None,
+                op0=mybir.AluOpType.mult,
+            )
+        pick_kp(3, 0, HALF)
+        nc.vector.tensor_copy(out=kp_planes[:, 3, HALF:O], in_=k1[3][:].indirect(offs3_sb[:, HALF // 16 : O // 16]))
         for h in range(2):
             nc.vector.quantize_mx(
                 out=a_codes[h][:].bitcast(FP8X4), scales=a_scales[h][:], in_=a_bf[h][:].rearrange("p j t -> p (j t)")
             )
-        pick_kp_vector(3, HALF, O)
-        pick_kp_scalar(3, 0, HALF)
-
+        for g in range(2):
+            nc.vector.tensor_copy(
+                out=kp_bf[g][:].rearrange("p (c i) t -> p c t i", i=4),
+                in_=kp_planes[:, :, g * HALF : (g + 1) * HALF].rearrange("p t (c i) -> p c t i", i=4),
+            )
+        out_view = out.rearrange("(h p) (g o) -> g p h o", h=2, g=2)
         for g in range(2):
             nc.vector.quantize_mx(
-                out=kp_codes[g][:].bitcast(FP8X4),
-                scales=kp_scales[g][:],
-                in_=kp_bf[:, PACK * HALF * g : PACK * HALF * (g + 1)],
+                out=kp_codes[g][:].bitcast(FP8X4), scales=kp_scales[g][:], in_=kp_bf[g][:].rearrange("p o t -> p (o t)")
             )
+        for g in range(2):
             for h in range(2):
                 nc.tensor.matmul_mx(
-                    out=out_ps[h][:, g * HALF : (g + 1) * HALF],
+                    out=out_ps[g][h][:],
                     lhsT=a_codes[h][:].bitcast(FP8X4),
                     lhsT_scale=a_scales[h][:],
                     rhs=kp_codes[g][:].bitcast(FP8X4),
@@ -156,8 +161,6 @@ def tile_list_twolevels_kernel(tc, xt_words, xt_scales, w_words, w_scales, ca, s
                     start=True,
                     stop=True,
                 )
-
-        nc.scalar.copy(out=out_sb[0][:], in_=out_ps[0][:])
-        nc.scalar.dma_start(out=out[0:HALF, :], in_=out_sb[0][:])
-        nc.vector.tensor_copy(out=out_sb[1][:], in_=out_ps[1][:])
-        nc.sync.dma_start(out=out[HALF:J, :], in_=out_sb[1][:])
+            nc.scalar.copy(out=out_sb[g][:, 0, :], in_=out_ps[g][0][:])
+            nc.vector.tensor_copy(out=out_sb[g][:, 1, :], in_=out_ps[g][1][:])
+            nc.sync.dma_start(out=out_view[g], in_=out_sb[g][:])

@@ -35,7 +35,7 @@ def tile_list_twolevels_kernel(tc, xt_words, xt_scales, w_words, w_scales, ca, s
         ca_sb = [keep.tile([P, D], U8, name=f"ca_sb{t}") for t in range(PACK)]
         ca_picked = [keep.tile([P, U], U8, name=f"ca_picked{t}") for t in range(PACK)]
         k1 = [keep.tile([P, U], F32, name=f"k1_{t}") for t in range(PACK)]
-        st_sb = keep.tile([P, PACK], F32, name="st_sb")
+        st_sb = keep.tile([P, 7], F32, name="st_sb")
         xw_sb = keep.tile([P, T], I32, name="xw_sb")
         xs_sb = keep.tile([P, T], U8, name="xs_sb")
         xw_picked = keep.tile([P, J], U32, name="xw_picked", align_bytes=64)
@@ -57,7 +57,7 @@ def tile_list_twolevels_kernel(tc, xt_words, xt_scales, w_words, w_scales, ca, s
         out_ps = [[psum.tile([P, HALF], F32, name=f"out_ps{g}{h}") for h in range(2)] for g in range(2)]
 
         ca_rows = ca.rearrange("(c t e) d -> t c e d", t=PACK, e=2)
-        st_rows = st.rearrange("(c t e) o -> e c (t o)", t=PACK, e=2)
+        st_rows = st.rearrange("(c s) o -> c (s o)", s=8)
 
         def load_scale_rows(queue, plane, rows):
             for r in range(4):
@@ -66,19 +66,18 @@ def tile_list_twolevels_kernel(tc, xt_words, xt_scales, w_words, w_scales, ca, s
         nc.vector.memset(ws_sb[:].bitcast(I32), 0)
         nc.vector.memset(xs_sb[:].bitcast(I32), 0)
 
-        nc.sync.dma_start(offs2_sb[:], offs2)
         nc.scalar.dma_start(out=ws_rows[:].bitcast(I32), in_=w_scales[0].rearrange("(q r) c -> r q c", r=4).bitcast(I32))
+        for e in range(2):
+            nc.scalar.dma_start(out=st_sb[e:P:2, :], in_=st_rows[:, e : e + 7])
+        nc.sync.dma_start(offs2_sb[:], offs2)
         nc.sync.dma_start(out=ca_sb[0][:], in_=ca_rows[0])
         nc.sync.dma_start(out=ww_sb[:].bitcast(I32), in_=w_words[0].bitcast(I32))
         nc.sync.dma_start(out=ca_sb[1][:], in_=ca_rows[1])
-        with nc.allow_non_contiguous_dma(reason="one step for each partition and plane"):
-            for e in range(2):
-                nc.sync.dma_start(out=st_sb[e:P:2, :], in_=st_rows[e])
         nc.sync.dma_start(offs3_sb[:], offs3)
         nc.sync.dma_start(out=ca_sb[2][:], in_=ca_rows[2])
-        nc.sync.dma_start(out=xw_sb[:], in_=xt_words[0].rearrange("p n t -> p (n t)").bitcast(I32))
         nc.sync.dma_start(offs_sb[:], offs)
         load_scale_rows(nc.sync, xs_sb, xt_scales)
+        nc.sync.dma_start(out=xw_sb[:], in_=xt_words[0].rearrange("p n t -> p (n t)").bitcast(I32))
         nc.sync.dma_start(out=ca_sb[3][:], in_=ca_rows[3])
 
         for q in range(4):
@@ -96,20 +95,23 @@ def tile_list_twolevels_kernel(tc, xt_words, xt_scales, w_words, w_scales, ca, s
             nc.vector.tensor_copy(out=ca_picked[t][:, lo:hi], in_=ca_sb[t][:].indirect(offs2_sb[:, lo // 16 : hi // 16]))
 
         def make_k1(t, lo, hi):
-            nc.scalar.activation(out=k1[t][:, lo:hi], in_=ca_picked[t][:, lo:hi].bitcast(FP8), func=COPY, scale=st_sb[:, t : t + 1])
+            nc.scalar.activation(out=k1[t][:, lo:hi], in_=ca_picked[t][:, lo:hi].bitcast(FP8), func=COPY, scale=st_sb[:, 2 * t : 2 * t + 1])
 
         def pick_kp(t, lo, hi):
             nc.scalar.activation(out=kp_planes[:, t, lo:hi], in_=k1[t][:].indirect(offs3_sb[:, lo // 16 : hi // 16]), func=COPY)
 
         for t in range(3):
-            pick_codes(t, 0, U)
-            make_k1(t, 0, U)
+            pieces = 2 if t == 0 else 1
+            for i in range(pieces):
+                pick_codes(t, i * U // pieces, (i + 1) * U // pieces)
+                make_k1(t, i * U // pieces, (i + 1) * U // pieces)
             pick_kp(t, 0, O)
 
-        nc.vector.tensor_copy(out=xw_picked[:], in_=xw_sb[:].bitcast(U32).indirect(offs_sb[:]))
         nc.vector.tensor_copy(out=xs_picked[:], in_=xs_sb[:].indirect(offs_sb[:]))
         for h in range(2):
             cols = slice(h * HALF, (h + 1) * HALF)
+            slots = offs_sb[:, h * HALF // 16 : (h + 1) * HALF // 16]
+            nc.vector.tensor_copy(out=xw_picked[:, cols], in_=xw_sb[:].bitcast(U32).indirect(slots))
             for t in range(PACK):
                 nc.tensor.matmul_mx(
                     out=a_ps[h][:, t, :],
@@ -130,7 +132,7 @@ def tile_list_twolevels_kernel(tc, xt_words, xt_scales, w_words, w_scales, ca, s
             nc.vector.tensor_scalar(
                 out=k1[3][:, lo : lo + U // 2],
                 in0=ca_picked[3][:, lo : lo + U // 2].bitcast(FP8),
-                scalar1=st_sb[:, 3:4],
+                scalar1=st_sb[:, 6:7],
                 scalar2=None,
                 op0=mybir.AluOpType.mult,
             )
@@ -140,17 +142,17 @@ def tile_list_twolevels_kernel(tc, xt_words, xt_scales, w_words, w_scales, ca, s
             nc.vector.quantize_mx(
                 out=a_codes[h][:].bitcast(FP8X4), scales=a_scales[h][:], in_=a_bf[h][:].rearrange("p j t -> p (j t)")
             )
-        for g in range(2):
-            nc.vector.tensor_copy(
+        for g, copy in enumerate((nc.scalar.copy, nc.vector.tensor_copy)):
+            copy(
                 out=kp_bf[g][:].rearrange("p (c i) t -> p c t i", i=4),
                 in_=kp_planes[:, :, g * HALF : (g + 1) * HALF].rearrange("p t (c i) -> p c t i", i=4),
             )
         out_view = out.rearrange("(h p) (g o) -> g p h o", h=2, g=2)
-        for g in range(2):
+        for g in (1, 0):
             nc.vector.quantize_mx(
                 out=kp_codes[g][:].bitcast(FP8X4), scales=kp_scales[g][:], in_=kp_bf[g][:].rearrange("p o t -> p (o t)")
             )
-        for g in range(2):
+        for g in (1, 0):
             for h in range(2):
                 nc.tensor.matmul_mx(
                     out=out_ps[g][h][:],

@@ -48,8 +48,7 @@ def tile_list_twolevels_kernel(tc, xt_words, xt_scales, w_words, w_scales, ca, s
         a_bf = [keep.tile([P, HALF, PACK], BF16, name=f"a_bf{h}", align_bytes=64) for h in range(2)]
         a_codes = [keep.tile([P, HALF], U32, name=f"a_codes{h}", align_bytes=64) for h in range(2)]
         a_scales = [keep.tile([P, HALF], U8, name=f"a_scales{h}", align_bytes=64) for h in range(2)]
-        kp_planes = keep.tile([P, PACK, O], BF16, name="kp_planes")
-        kp_bf = [keep.tile([P, HALF, PACK], BF16, name=f"kp_bf{h}", align_bytes=64) for h in range(2)]
+        kp_bf = keep.tile([P, O * PACK], BF16, name="kp_bf", align_bytes=64)
         kp_codes = [keep.tile([P, HALF], U32, name=f"kp_codes{h}", align_bytes=64) for h in range(2)]
         kp_scales = [keep.tile([P, HALF], U8, name=f"kp_scales{h}", align_bytes=64) for h in range(2)]
         out_sb = [keep.tile([P, 2, HALF], F32, name=f"out_sb{g}") for g in range(2)]
@@ -98,7 +97,7 @@ def tile_list_twolevels_kernel(tc, xt_words, xt_scales, w_words, w_scales, ca, s
             nc.scalar.activation(out=k1[t][:, lo:hi], in_=ca_picked[t][:, lo:hi].bitcast(FP8), func=COPY, scale=st_sb[:, 2 * t : 2 * t + 1])
 
         def pick_kp(t, lo, hi):
-            nc.scalar.activation(out=kp_planes[:, t, lo:hi], in_=k1[t][:].indirect(offs3_sb[:, lo // 16 : hi // 16]), func=COPY)
+            nc.scalar.activation(out=kp_bf[:, PACK * lo + t : PACK * hi : PACK], in_=k1[t][:].indirect(offs3_sb[:, lo // 16 : hi // 16]), func=COPY)
 
         for t in range(3):
             pieces = 2 if t == 0 else 1
@@ -136,21 +135,16 @@ def tile_list_twolevels_kernel(tc, xt_words, xt_scales, w_words, w_scales, ca, s
                 scalar2=None,
                 op0=mybir.AluOpType.mult,
             )
-        pick_kp(3, 0, HALF)
-        nc.vector.tensor_copy(out=kp_planes[:, 3, HALF:O], in_=k1[3][:].indirect(offs3_sb[:, HALF // 16 : O // 16]))
         for h in range(2):
             nc.vector.quantize_mx(
                 out=a_codes[h][:].bitcast(FP8X4), scales=a_scales[h][:], in_=a_bf[h][:].rearrange("p j t -> p (j t)")
             )
-        for g, copy in enumerate((nc.scalar.copy, nc.vector.tensor_copy)):
-            copy(
-                out=kp_bf[g][:].rearrange("p (c i) t -> p c t i", i=4),
-                in_=kp_planes[:, :, g * HALF : (g + 1) * HALF].rearrange("p t (c i) -> p c t i", i=4),
-            )
+        pick_kp(3, 0, HALF)
+        nc.vector.tensor_copy(out=kp_bf[:, PACK * HALF + 3 : PACK * O : PACK], in_=k1[3][:].indirect(offs3_sb[:, HALF // 16 : O // 16]))
         out_view = out.rearrange("(h p) (g o) -> g p h o", h=2, g=2)
         for g in (1, 0):
             nc.vector.quantize_mx(
-                out=kp_codes[g][:].bitcast(FP8X4), scales=kp_scales[g][:], in_=kp_bf[g][:].rearrange("p o t -> p (o t)")
+                out=kp_codes[g][:].bitcast(FP8X4), scales=kp_scales[g][:], in_=kp_bf[:, PACK * HALF * g : PACK * HALF * (g + 1)]
             )
         for g in (1, 0):
             for h in range(2):
@@ -164,5 +158,6 @@ def tile_list_twolevels_kernel(tc, xt_words, xt_scales, w_words, w_scales, ca, s
                     stop=True,
                 )
             nc.scalar.copy(out=out_sb[g][:, 0, :], in_=out_ps[g][0][:])
-            nc.vector.tensor_copy(out=out_sb[g][:, 1, :], in_=out_ps[g][1][:])
+            copy = nc.scalar.copy if g == 1 else nc.vector.tensor_copy
+            copy(out=out_sb[g][:, 1, :], in_=out_ps[g][1][:])
             nc.sync.dma_start(out=out_view[g], in_=out_sb[g][:])

@@ -17,8 +17,13 @@ FP4X4 = mybir.dt.float4_e2m1fn_x4
 COPY = mybir.ActivationFunctionType.Copy
 
 P = 128
-PACK = 4
+PLANES = 4
+LAST = PLANES - 1
 HALF = 128
+QUADS = 4
+QUAD_ROWS = 4
+PER_COLUMN = 16
+STEP_RUN = 2 * PLANES - 1
 
 
 def tile_list_twolevels_kernel(tc, xt_words, xt_scales, w_words, w_scales, ca, st, offs, offs2, offs3, out):
@@ -28,110 +33,122 @@ def tile_list_twolevels_kernel(tc, xt_words, xt_scales, w_words, w_scales, ca, s
         keep = ctx.enter_context(tc.tile_pool(name="keep", bufs=1))
         psum = ctx.enter_context(tc.psum_pool(name="psum", bufs=1))
 
-        offs_sb = lists.tile([P, J // 16], U16, name="offs_sb")
-        offs2_sb = lists.tile([P, U // 16], U16, name="offs2_sb")
-        offs3_sb = lists.tile([P, O // 16], U16, name="offs3_sb")
+        offs_sb = lists.tile([P, J // PER_COLUMN], U16, name="offs_sb")
+        offs2_sb = lists.tile([P, U // PER_COLUMN], U16, name="offs2_sb")
+        offs3_sb = lists.tile([P, O // PER_COLUMN], U16, name="offs3_sb")
 
-        ca_sb = [keep.tile([P, D], U8, name=f"ca_sb{t}") for t in range(PACK)]
-        ca_picked = [keep.tile([P, U], U8, name=f"ca_picked{t}") for t in range(PACK)]
-        k1 = [keep.tile([P, U], F32, name=f"k1_{t}") for t in range(PACK)]
-        st_sb = keep.tile([P, 7], F32, name="st_sb")
+        ca_sb = [keep.tile([P, D], U8, name=f"ca_sb{t}") for t in range(PLANES)]
+        ca_picked = [keep.tile([P, U], U8, name=f"ca_picked{t}") for t in range(PLANES)]
+        k1 = [keep.tile([P, U], F32, name=f"k1_{t}") for t in range(PLANES)]
+        st_sb = keep.tile([P, STEP_RUN], F32, name="st_sb")
         xw_sb = keep.tile([P, T], I32, name="xw_sb")
         xs_sb = keep.tile([P, T], U8, name="xs_sb")
         xw_picked = keep.tile([P, J], U32, name="xw_picked", align_bytes=64)
         xs_picked = keep.tile([P, J], U8, name="xs_picked", align_bytes=64)
         ww_sb = keep.tile([P, 2 * R], U8, name="ww_sb")
         ws_sb = keep.tile([P, R], U8, name="ws_sb")
-        ws_rows = keep.tile([4, 4, R], U8, name="ws_rows")
+        ws_rows = keep.tile([QUAD_ROWS, QUADS, R], U8, name="ws_rows")
         ww_dealt = keep.tile([P, 2 * R], U8, name="ww_dealt", align_bytes=64)
         ws_dealt = keep.tile([P, R], U8, name="ws_dealt", align_bytes=64)
-        a_bf = [keep.tile([P, HALF, PACK], BF16, name=f"a_bf{h}", align_bytes=64) for h in range(2)]
+        a_bf = [keep.tile([P, HALF, PLANES], BF16, name=f"a_bf{h}", align_bytes=64) for h in range(2)]
         a_codes = [keep.tile([P, HALF], U32, name=f"a_codes{h}", align_bytes=64) for h in range(2)]
         a_scales = [keep.tile([P, HALF], U8, name=f"a_scales{h}", align_bytes=64) for h in range(2)]
-        kp_bf = keep.tile([P, O * PACK], BF16, name="kp_bf", align_bytes=64)
-        kp_codes = [keep.tile([P, HALF], U32, name=f"kp_codes{h}", align_bytes=64) for h in range(2)]
-        kp_scales = [keep.tile([P, HALF], U8, name=f"kp_scales{h}", align_bytes=64) for h in range(2)]
+        kp_pairs = keep.tile([P, 2, 2 * O], BF16, name="kp_pairs")
+        kp_bf = [keep.tile([P, HALF * PLANES], BF16, name=f"kp_bf{g}", align_bytes=64) for g in range(2)]
+        kp_codes = [keep.tile([P, HALF], U32, name=f"kp_codes{g}", align_bytes=64) for g in range(2)]
+        kp_scales = [keep.tile([P, HALF], U8, name=f"kp_scales{g}", align_bytes=64) for g in range(2)]
         out_sb = [keep.tile([P, 2, HALF], F32, name=f"out_sb{g}") for g in range(2)]
-        a_ps = [psum.tile([P, PACK, HALF], F32, name=f"a_ps{h}") for h in range(2)]
+        a_ps = [psum.tile([P, PLANES, HALF], F32, name=f"a_ps{h}") for h in range(2)]
         out_ps = [[psum.tile([P, HALF], F32, name=f"out_ps{g}{h}") for h in range(2)] for g in range(2)]
 
-        ca_rows = ca.rearrange("(c t e) d -> t c e d", t=PACK, e=2)
-        st_rows = st.rearrange("(c s) o -> c (s o)", s=8)
-
-        def load_scale_rows(queue, plane, rows):
-            for r in range(4):
-                queue.dma_start(out=plane[r:P:32, :].bitcast(I32), in_=rows[0, r:16:4, :].bitcast(I32))
+        def entries(list_tile, lo, hi):
+            return list_tile[:, lo // PER_COLUMN : hi // PER_COLUMN]
 
         nc.vector.memset(ws_sb[:].bitcast(I32), 0)
         nc.vector.memset(xs_sb[:].bitcast(I32), 0)
 
-        nc.scalar.dma_start(out=ws_rows[:].bitcast(I32), in_=w_scales[0].rearrange("(q r) c -> r q c", r=4).bitcast(I32))
-        for e in range(2):
-            nc.scalar.dma_start(out=st_sb[e:P:2, :], in_=st_rows[:, e : e + 7])
+        ca_planes = ca.rearrange("(c t e) d -> t c e d", t=PLANES, e=2)
+        st_runs = st.rearrange("(c s) o -> c (s o)", s=2 * PLANES)
         nc.sync.dma_start(offs2_sb[:], offs2)
-        nc.sync.dma_start(out=ca_sb[0][:], in_=ca_rows[0])
+        nc.scalar.dma_start(
+            out=ws_rows[:].bitcast(I32), in_=w_scales[0].rearrange("(q s) c -> s q c", s=QUAD_ROWS).bitcast(I32)
+        )
+        for e in range(2):
+            nc.scalar.dma_start(out=st_sb[e:P:2, :], in_=st_runs[:, e : e + STEP_RUN])
+        nc.sync.dma_start(out=ca_sb[0][:], in_=ca_planes[0])
         nc.sync.dma_start(out=ww_sb[:].bitcast(I32), in_=w_words[0].bitcast(I32))
-        nc.sync.dma_start(out=ca_sb[1][:], in_=ca_rows[1])
+        nc.sync.dma_start(out=ca_sb[1][:], in_=ca_planes[1])
         nc.sync.dma_start(offs3_sb[:], offs3)
-        nc.sync.dma_start(out=ca_sb[2][:], in_=ca_rows[2])
+        nc.sync.dma_start(out=ca_sb[2][:], in_=ca_planes[2])
         nc.sync.dma_start(offs_sb[:], offs)
-        load_scale_rows(nc.sync, xs_sb, xt_scales)
-        nc.sync.dma_start(out=xw_sb[:], in_=xt_words[0].rearrange("p n t -> p (n t)").bitcast(I32))
-        nc.sync.dma_start(out=ca_sb[3][:], in_=ca_rows[3])
+        for s in range(QUAD_ROWS):
+            nc.sync.dma_start(
+                out=xs_sb[s : P : P // QUADS, :].bitcast(I32),
+                in_=xt_scales[0, s : QUADS * QUAD_ROWS : QUAD_ROWS, :].bitcast(I32),
+            )
+        nc.sync.dma_start(out=xw_sb[:], in_=xt_words[0].rearrange("p n i -> p (n i)").bitcast(I32))
+        nc.sync.dma_start(out=ca_sb[LAST][:], in_=ca_planes[LAST])
 
-        for q in range(4):
-            nc.vector.tensor_copy(out=ws_sb[32 * q : 32 * q + 4, :].bitcast(I32), in_=ws_rows[:, q, :].bitcast(I32))
+        for q in range(QUADS):
+            first = q * (P // QUADS)
+            nc.vector.tensor_copy(out=ws_sb[first : first + QUAD_ROWS, :].bitcast(I32), in_=ws_rows[:, q, :].bitcast(I32))
         nc.scalar.copy(
-            out=ww_dealt[:].bitcast(U32).rearrange("p (t c) -> p t c", t=PACK),
-            in_=ww_sb[:].bitcast(U32).rearrange("p (c t) -> p t c", t=PACK),
+            out=ww_dealt[:].bitcast(U32).rearrange("p (t c) -> p t c", t=PLANES),
+            in_=ww_sb[:].bitcast(U32).rearrange("p (c t) -> p t c", t=PLANES),
         )
         nc.scalar.copy(
-            out=ws_dealt[:].bitcast(U16).rearrange("p (t c) -> p t c", t=PACK),
-            in_=ws_sb[:].bitcast(U16).rearrange("p (c t) -> p t c", t=PACK),
+            out=ws_dealt[:].bitcast(U16).rearrange("p (t c) -> p t c", t=PLANES),
+            in_=ws_sb[:].bitcast(U16).rearrange("p (c t) -> p t c", t=PLANES),
         )
 
-        def pick_codes(t, lo, hi):
-            nc.vector.tensor_copy(out=ca_picked[t][:, lo:hi], in_=ca_sb[t][:].indirect(offs2_sb[:, lo // 16 : hi // 16]))
+        def pick_bytes(t, lo, hi):
+            nc.vector.tensor_copy(out=ca_picked[t][:, lo:hi], in_=ca_sb[t][:].indirect(entries(offs2_sb, lo, hi)))
 
-        def make_k1(t, lo, hi):
-            nc.scalar.activation(out=k1[t][:, lo:hi], in_=ca_picked[t][:, lo:hi].bitcast(FP8), func=COPY, scale=st_sb[:, 2 * t : 2 * t + 1])
+        def step_of(t):
+            return st_sb[:, 2 * t : 2 * t + 1]
 
-        def pick_kp(t, lo, hi):
-            nc.scalar.activation(out=kp_bf[:, PACK * lo + t : PACK * hi : PACK], in_=k1[t][:].indirect(offs3_sb[:, lo // 16 : hi // 16]), func=COPY)
+        def kp_slot(t, lo, hi):
+            return kp_pairs[:, t // 2, 2 * lo + t % 2 : 2 * hi : 2]
 
-        for t in range(3):
+        def picked_k1(t, lo, hi):
+            return k1[t][:].indirect(entries(offs3_sb, lo, hi))
+
+        for t in range(LAST):
             pieces = 2 if t == 0 else 1
             for i in range(pieces):
-                pick_codes(t, i * U // pieces, (i + 1) * U // pieces)
-                make_k1(t, i * U // pieces, (i + 1) * U // pieces)
-            pick_kp(t, 0, O)
+                lo, hi = i * U // pieces, (i + 1) * U // pieces
+                pick_bytes(t, lo, hi)
+                nc.scalar.activation(
+                    out=k1[t][:, lo:hi], in_=ca_picked[t][:, lo:hi].bitcast(FP8), func=COPY, scale=step_of(t)
+                )
+            nc.scalar.activation(out=kp_slot(t, 0, O), in_=picked_k1(t, 0, O), func=COPY)
 
         nc.vector.tensor_copy(out=xs_picked[:], in_=xs_sb[:].indirect(offs_sb[:]))
         for h in range(2):
-            cols = slice(h * HALF, (h + 1) * HALF)
-            slots = offs_sb[:, h * HALF // 16 : (h + 1) * HALF // 16]
-            nc.vector.tensor_copy(out=xw_picked[:, cols], in_=xw_sb[:].bitcast(U32).indirect(slots))
-            for t in range(PACK):
+            lo, hi = h * HALF, (h + 1) * HALF
+            nc.vector.tensor_copy(out=xw_picked[:, lo:hi], in_=xw_sb[:].bitcast(U32).indirect(entries(offs_sb, lo, hi)))
+            for t in range(PLANES):
                 nc.tensor.matmul_mx(
                     out=a_ps[h][:, t, :],
                     lhsT=ww_dealt[:, 2 * P * t : 2 * P * (t + 1)].bitcast(FP4X4),
                     lhsT_scale=ws_dealt[:, P * t : P * (t + 1)],
-                    rhs=xw_picked[:, cols].bitcast(FP8X4),
-                    rhs_scale=xs_picked[:, cols],
+                    rhs=xw_picked[:, lo:hi].bitcast(FP8X4),
+                    rhs_scale=xs_picked[:, lo:hi],
                     start=True,
                     stop=True,
                 )
 
-        pick_codes(3, 0, U // 2)
-        pick_codes(3, U // 2, U)
+        for lo in (0, U // 2):
+            pick_bytes(LAST, lo, lo + U // 2)
 
         for h in range(2):
             nc.scalar.copy(out=a_bf[h][:], in_=a_ps[h][:].rearrange("p t j -> p j t"))
+
         for lo in (0, U // 2):
             nc.vector.tensor_scalar(
-                out=k1[3][:, lo : lo + U // 2],
-                in0=ca_picked[3][:, lo : lo + U // 2].bitcast(FP8),
-                scalar1=st_sb[:, 6:7],
+                out=k1[LAST][:, lo : lo + U // 2],
+                in0=ca_picked[LAST][:, lo : lo + U // 2].bitcast(FP8),
+                scalar1=step_of(LAST),
                 scalar2=None,
                 op0=mybir.AluOpType.mult,
             )
@@ -139,14 +156,20 @@ def tile_list_twolevels_kernel(tc, xt_words, xt_scales, w_words, w_scales, ca, s
             nc.vector.quantize_mx(
                 out=a_codes[h][:].bitcast(FP8X4), scales=a_scales[h][:], in_=a_bf[h][:].rearrange("p j t -> p (j t)")
             )
-        pick_kp(3, 0, HALF)
-        nc.vector.tensor_copy(out=kp_bf[:, PACK * HALF + 3 : PACK * O : PACK], in_=k1[3][:].indirect(offs3_sb[:, HALF // 16 : O // 16]))
-        out_view = out.rearrange("(h p) (g o) -> g p h o", h=2, g=2)
-        for g in (1, 0):
-            nc.vector.quantize_mx(
-                out=kp_codes[g][:].bitcast(FP8X4), scales=kp_scales[g][:], in_=kp_bf[:, PACK * HALF * g : PACK * HALF * (g + 1)]
+        nc.scalar.activation(out=kp_slot(LAST, 0, HALF), in_=picked_k1(LAST, 0, HALF), func=COPY)
+        nc.vector.tensor_copy(out=kp_slot(LAST, HALF, O), in_=picked_k1(LAST, HALF, O))
+
+        read_halves = (1, 0)
+        for g in read_halves:
+            nc.vector.tensor_copy(
+                out=kp_bf[g][:].bitcast(I32).rearrange("p (o u) -> p o u", u=2),
+                in_=kp_pairs[:].bitcast(I32)[:, :, g * HALF : (g + 1) * HALF].rearrange("p u o -> p o u"),
             )
-        for g in (1, 0):
+        for g in read_halves:
+            nc.vector.quantize_mx(out=kp_codes[g][:].bitcast(FP8X4), scales=kp_scales[g][:], in_=kp_bf[g][:])
+
+        out_halves = out.rearrange("(h p) (g o) -> g p h o", h=2, g=2)
+        for g in read_halves:
             for h in range(2):
                 nc.tensor.matmul_mx(
                     out=out_ps[g][h][:],
@@ -157,7 +180,7 @@ def tile_list_twolevels_kernel(tc, xt_words, xt_scales, w_words, w_scales, ca, s
                     start=True,
                     stop=True,
                 )
+            second_copy = nc.scalar.copy if g == read_halves[0] else nc.vector.tensor_copy
             nc.scalar.copy(out=out_sb[g][:, 0, :], in_=out_ps[g][0][:])
-            copy = nc.scalar.copy if g == 1 else nc.vector.tensor_copy
-            copy(out=out_sb[g][:, 1, :], in_=out_ps[g][1][:])
-            nc.sync.dma_start(out=out_view[g], in_=out_sb[g][:])
+            second_copy(out=out_sb[g][:, 1, :], in_=out_ps[g][1][:])
+            nc.sync.dma_start(out=out_halves[g], in_=out_sb[g][:])

from contextlib import ExitStack

import concourse.mybir as mybir

K, T, J, R, D, U, O = 512, 1024, 256, 512, 2048, 512, 256
FLOPS = 2 * K * R * J + 2 * R * J * O

F32 = mybir.dt.float32
BF16 = mybir.dt.bfloat16
I32 = mybir.dt.int32
U32 = mybir.dt.uint32
U16 = mybir.dt.uint16
U8 = mybir.dt.uint8
FP8 = mybir.dt.float8_e4m3fn
FP8X4 = mybir.dt.float8_e4m3fn_x4
FP4X4 = mybir.dt.float4_e2m1fn_x4
COPY = mybir.ActivationFunctionType.Copy

P = 128
PLANES = 4
LAST = PLANES - 1
HALF = 128
QUADS = 4
QUAD_ROWS = 4
PER_COLUMN = 16
STEP_RUN = 2 * PLANES - 1


def tile_list_twolevels_kernel(tc, xt_words, xt_scales, w_words, w_scales, ca, st, offs, offs2, offs3, out):
    nc = tc.nc
    with ExitStack() as ctx:
        lists = ctx.enter_context(tc.tile_pool(name="lists", bufs=1))
        keep = ctx.enter_context(tc.tile_pool(name="keep", bufs=1))
        psum = ctx.enter_context(tc.psum_pool(name="psum", bufs=1))

        offs_sb = lists.tile([P, J // PER_COLUMN], U16, name="offs_sb")
        offs2_sb = lists.tile([P, U // PER_COLUMN], U16, name="offs2_sb")
        offs3_sb = lists.tile([P, O // PER_COLUMN], U16, name="offs3_sb")

        ca_sb = [keep.tile([P, D], U8, name=f"ca_sb{t}") for t in range(PLANES)]
        ca_picked = [keep.tile([P, U], U8, name=f"ca_picked{t}") for t in range(PLANES)]
        k1 = [keep.tile([P, U], F32, name=f"k1_{t}") for t in range(PLANES)]
        st_sb = keep.tile([P, STEP_RUN], F32, name="st_sb")
        xw_sb = keep.tile([P, T], I32, name="xw_sb")
        xs_sb = keep.tile([P, T], U8, name="xs_sb")
        xw_picked = keep.tile([P, J], U32, name="xw_picked", align_bytes=64)
        xs_picked = keep.tile([P, J], U8, name="xs_picked", align_bytes=64)
        ww_sb = keep.tile([P, 2 * R], U8, name="ww_sb")
        ws_sb = keep.tile([P, R], U8, name="ws_sb")
        ws_rows = keep.tile([QUAD_ROWS, QUADS, R], U8, name="ws_rows")
        ww_dealt = keep.tile([P, 2 * R], U8, name="ww_dealt", align_bytes=64)
        ws_dealt = keep.tile([P, R], U8, name="ws_dealt", align_bytes=64)
        a_bf = [keep.tile([P, HALF, PLANES], BF16, name=f"a_bf{h}", align_bytes=64) for h in range(2)]
        a_codes = [keep.tile([P, HALF], U32, name=f"a_codes{h}", align_bytes=64) for h in range(2)]
        a_scales = [keep.tile([P, HALF], U8, name=f"a_scales{h}", align_bytes=64) for h in range(2)]
        kp_pairs = keep.tile([P, 2, 2 * O], BF16, name="kp_pairs")
        kp_bf = [keep.tile([P, HALF * PLANES], BF16, name=f"kp_bf{g}", align_bytes=64) for g in range(2)]
        kp_codes = [keep.tile([P, HALF], U32, name=f"kp_codes{g}", align_bytes=64) for g in range(2)]
        kp_scales = [keep.tile([P, HALF], U8, name=f"kp_scales{g}", align_bytes=64) for g in range(2)]
        out_sb = [keep.tile([P, 2, HALF], F32, name=f"out_sb{g}") for g in range(2)]
        a_ps = [psum.tile([P, PLANES, HALF], F32, name=f"a_ps{h}") for h in range(2)]
        out_ps = [[psum.tile([P, HALF], F32, name=f"out_ps{g}{h}") for h in range(2)] for g in range(2)]

        def entries(list_tile, lo, hi):
            return list_tile[:, lo // PER_COLUMN : hi // PER_COLUMN]

        nc.vector.memset(ws_sb[:].bitcast(I32), 0)
        nc.vector.memset(xs_sb[:].bitcast(I32), 0)

        ca_planes = ca.rearrange("(c t e) d -> t c e d", t=PLANES, e=2)
        st_runs = st.rearrange("(c s) o -> c (s o)", s=2 * PLANES)
        nc.sync.dma_start(offs2_sb[:], offs2)
        nc.scalar.dma_start(
            out=ws_rows[:].bitcast(I32), in_=w_scales[0].rearrange("(q s) c -> s q c", s=QUAD_ROWS).bitcast(I32)
        )
        for e in range(2):
            nc.scalar.dma_start(out=st_sb[e:P:2, :], in_=st_runs[:, e : e + STEP_RUN])
        nc.sync.dma_start(out=ca_sb[0][:], in_=ca_planes[0])
        nc.sync.dma_start(out=ww_sb[:].bitcast(I32), in_=w_words[0].bitcast(I32))
        nc.sync.dma_start(out=ca_sb[1][:], in_=ca_planes[1])
        nc.sync.dma_start(offs3_sb[:], offs3)
        nc.sync.dma_start(out=ca_sb[2][:], in_=ca_planes[2])
        nc.sync.dma_start(offs_sb[:], offs)
        for s in range(QUAD_ROWS):
            nc.sync.dma_start(
                out=xs_sb[s : P : P // QUADS, :].bitcast(I32),
                in_=xt_scales[0, s : QUADS * QUAD_ROWS : QUAD_ROWS, :].bitcast(I32),
            )
        nc.sync.dma_start(out=xw_sb[:], in_=xt_words[0].rearrange("p n i -> p (n i)").bitcast(I32))
        nc.sync.dma_start(out=ca_sb[LAST][:], in_=ca_planes[LAST])

        for q in range(QUADS):
            first = q * (P // QUADS)
            nc.vector.tensor_copy(out=ws_sb[first : first + QUAD_ROWS, :].bitcast(I32), in_=ws_rows[:, q, :].bitcast(I32))
        nc.scalar.copy(
            out=ww_dealt[:].bitcast(U32).rearrange("p (t c) -> p t c", t=PLANES),
            in_=ww_sb[:].bitcast(U32).rearrange("p (c t) -> p t c", t=PLANES),
        )
        nc.scalar.copy(
            out=ws_dealt[:].bitcast(U16).rearrange("p (t c) -> p t c", t=PLANES),
            in_=ws_sb[:].bitcast(U16).rearrange("p (c t) -> p t c", t=PLANES),
        )

        def pick_bytes(t, lo, hi):
            nc.vector.tensor_copy(out=ca_picked[t][:, lo:hi], in_=ca_sb[t][:].indirect(entries(offs2_sb, lo, hi)))

        def step_of(t):
            return st_sb[:, 2 * t : 2 * t + 1]

        def kp_slot(t, lo, hi):
            return kp_pairs[:, t // 2, 2 * lo + t % 2 : 2 * hi : 2]

        def picked_k1(t, lo, hi):
            return k1[t][:].indirect(entries(offs3_sb, lo, hi))

        for t in range(LAST):
            pieces = 2 if t == 0 else 1
            for i in range(pieces):
                lo, hi = i * U // pieces, (i + 1) * U // pieces
                pick_bytes(t, lo, hi)
                nc.scalar.activation(
                    out=k1[t][:, lo:hi], in_=ca_picked[t][:, lo:hi].bitcast(FP8), func=COPY, scale=step_of(t)
                )
            nc.scalar.activation(out=kp_slot(t, 0, O), in_=picked_k1(t, 0, O), func=COPY)

        nc.vector.tensor_copy(out=xs_picked[:], in_=xs_sb[:].indirect(offs_sb[:]))
        for h in range(2):
            lo, hi = h * HALF, (h + 1) * HALF
            nc.vector.tensor_copy(out=xw_picked[:, lo:hi], in_=xw_sb[:].bitcast(U32).indirect(entries(offs_sb, lo, hi)))
            for t in range(PLANES):
                nc.tensor.matmul_mx(
                    out=a_ps[h][:, t, :],
                    lhsT=ww_dealt[:, 2 * P * t : 2 * P * (t + 1)].bitcast(FP4X4),
                    lhsT_scale=ws_dealt[:, P * t : P * (t + 1)],
                    rhs=xw_picked[:, lo:hi].bitcast(FP8X4),
                    rhs_scale=xs_picked[:, lo:hi],
                    start=True,
                    stop=True,
                )

        for lo in (0, U // 2):
            pick_bytes(LAST, lo, lo + U // 2)

        for h in range(2):
            nc.scalar.copy(out=a_bf[h][:], in_=a_ps[h][:].rearrange("p t j -> p j t"))

        for lo in (0, U // 2):
            nc.vector.tensor_scalar(
                out=k1[LAST][:, lo : lo + U // 2],
                in0=ca_picked[LAST][:, lo : lo + U // 2].bitcast(FP8),
                scalar1=step_of(LAST),
                scalar2=None,
                op0=mybir.AluOpType.mult,
            )
        for h in range(2):
            nc.vector.quantize_mx(
                out=a_codes[h][:].bitcast(FP8X4), scales=a_scales[h][:], in_=a_bf[h][:].rearrange("p j t -> p (j t)")
            )
        nc.scalar.activation(out=kp_slot(LAST, 0, HALF), in_=picked_k1(LAST, 0, HALF), func=COPY)
        nc.vector.tensor_copy(out=kp_slot(LAST, HALF, O), in_=picked_k1(LAST, HALF, O))

        read_halves = (1, 0)
        for g in read_halves:
            nc.vector.tensor_copy(
                out=kp_bf[g][:].bitcast(I32).rearrange("p (o u) -> p o u", u=2),
                in_=kp_pairs[:].bitcast(I32)[:, :, g * HALF : (g + 1) * HALF].rearrange("p u o -> p o u"),
            )
        for g in read_halves:
            nc.vector.quantize_mx(out=kp_codes[g][:].bitcast(FP8X4), scales=kp_scales[g][:], in_=kp_bf[g][:])

        out_halves = out.rearrange("(h p) (g o) -> g p h o", h=2, g=2)
        for g in read_halves:
            for h in range(2):
                nc.tensor.matmul_mx(
                    out=out_ps[g][h][:],
                    lhsT=a_codes[h][:].bitcast(FP8X4),
                    lhsT_scale=a_scales[h][:],
                    rhs=kp_codes[g][:].bitcast(FP8X4),
                    rhs_scale=kp_scales[g][:],
                    start=True,
                    stop=True,
                )
            second_copy = nc.scalar.copy if g == read_halves[0] else nc.vector.tensor_copy
            nc.scalar.copy(out=out_sb[g][:, 0, :], in_=out_ps[g][0][:])
            second_copy(out=out_sb[g][:, 1, :], in_=out_ps[g][1][:])
            nc.sync.dma_start(out=out_halves[g], in_=out_sb[g][:])
